import numpy as np
import ml_dtypes


def mxq(x, axis, fmt="e4m3"):
    dtype, down = {"e4m3": (ml_dtypes.float8_e4m3fn, 7), "e5m2": (ml_dtypes.float8_e5m2, 14)}[fmt]
    v = np.moveaxis(np.asarray(x, np.float32).astype(ml_dtypes.bfloat16).astype(np.float64), axis, -1)
    blocks = v.reshape(v.shape[:-1] + (-1, 32))
    amax = np.abs(blocks).max(-1, keepdims=True)
    byte = np.maximum(np.where(amax > 0, np.frexp(amax)[1] - 1 + 127, 0) - down, 1)
    scale = np.exp2(byte - 127.0)
    codes = (blocks / scale).astype(np.float32).astype(dtype).astype(np.float64)
    return np.moveaxis((codes * scale).reshape(v.shape), -1, axis)


WIDE = False


def mx_kscale(k):
    if not WIDE:
        return np.ones(k)
    levels = np.array([10, -10, 5, -5, 0])
    if k % 512:
        return np.exp2(np.random.permutation(np.resize(levels, k // 32))).repeat(32)
    a = np.empty((k // 512, 16))
    for p in range(k // 512):
        a[p, :8] = np.random.permutation(np.resize(levels, 8))
        for g in range(8):
            far = levels[np.abs(levels - a[p, g]) >= 10]
            a[p, g + 8] = far[np.random.randint(len(far))]
    return np.exp2(a.ravel()).repeat(32)


def f64(x):
    return np.asarray(x).astype(np.float64)


def striped(idx):
    return np.tile(np.asarray(idx).reshape(-1, 16).T, (8, 1)).astype(np.uint16)


def unstriped(offs):
    return offs[:16].T.reshape(-1).astype(np.int64)


E2M1 = np.array([0.0, 0.5, 1.0, 1.5, 2.0, 3.0, 4.0, 6.0, -0.0, -0.5, -1.0, -1.5, -2.0, -3.0, -4.0, -6.0])


def pack_weight(w, fmt):
    k, n = w.shape
    w = f64(np.asarray(w, np.float32).astype(ml_dtypes.bfloat16)).reshape(k // 32, 32, n)
    amax = np.abs(w).max(1)
    if fmt == "e4m3":
        byte = np.frexp(amax)[1] - 1 + 127 - 7
    else:
        mant, ex = np.frexp(amax / 6.0)
        byte = np.where(mant > 0.5, ex, ex - 1) + 127
    byte = np.clip(np.where(amax > 0, byte, 1), 1, 254)
    scaled = (w * np.exp2(127.0 - byte)[:, None, :]).reshape(k, n).astype(np.float32)
    by_word = np.ascontiguousarray(scaled.reshape(k // 512, 128, 4, n).transpose(0, 1, 3, 2))
    if fmt == "e4m3":
        words = by_word.astype(ml_dtypes.float8_e4m3fn).view(np.uint8)
    else:
        c = by_word.astype(ml_dtypes.float4_e2m1fn).view(np.uint8) & 0xF
        words = (c[..., 0::2] | (c[..., 1::2] << 4)).reshape(k // 512, 128, 2 * n)
    return np.ascontiguousarray(words), np.ascontiguousarray(byte.astype(np.uint8).reshape(k // 512, 16, n))


def unpack_weight(words, scales, fmt):
    g, _, n = scales.shape
    words = np.ascontiguousarray(words).reshape(g, 128, n, -1)
    if fmt == "e4m3":
        vals = words.view(ml_dtypes.float8_e4m3fn).astype(np.float64)
    else:
        nib = np.empty((g, 128, n, 4), np.uint8)
        nib[..., 0::2] = words & 0xF
        nib[..., 1::2] = words >> 4
        vals = E2M1[nib]
    vals = vals * np.repeat(np.exp2(scales.astype(np.float64) - 127.0), 8, axis=1)[..., None]
    return vals.transpose(0, 1, 3, 2).reshape(g * 512, n)


D, K, R, T, I, Q, G = 512, 512, 512, 2048, 512, 128, 64


def setup_inputs():
    n = np.random.standard_normal
    idx = np.random.permutation(T)[:I]
    fd = mx_kscale(D)
    fk = mx_kscale(K)
    fr = mx_kscale(R)
    keysp = pack_weight(n((D, T)) / fd[:, None], "e4m3")
    tabp = pack_weight(n((K, T)) / fk[:, None], "e4m3")
    return {
        "query": (n((D, Q)) * 0.7 / np.sqrt(D) * fd[:, None]).astype(np.float32),
        "keys_words": keysp[0],
        "keys_scales": keysp[1],
        "tab_words": tabp[0],
        "tab_scales": tabp[1],
        "w1": (n((K, R)) * 1 / np.sqrt(K) * fk[:, None]).astype(np.float32),
        "temper": (np.random.uniform(0.4, 1.0, (R, 1))).astype(np.float32),
        "gout": (n((R, Q)) * 1 / np.sqrt(R) * fr[:, None]).astype(np.float32),
        "hsc": (np.random.uniform(0.7, 1.4, (R, 1)) / fr[:, None]).astype(np.float32),
        "old": (0.5 * n((Q, T))).astype(np.float32),
        "offs": striped(idx),
    }


def reference(query, keys_words, keys_scales, tab_words, tab_scales, w1, temper, gout, hsc, old, offs):
    idx = unstriped(offs)
    keysu = unpack_weight(keys_words, keys_scales, "e4m3")
    tabu = unpack_weight(tab_words, tab_scales, "e4m3")
    queryq = mxq(f64(query), 0, "e4m3")
    keysidxg = keysu[:, idx]
    a = queryq.T @ keysidxg
    p = np.exp(a - np.max(a, axis=1, keepdims=True))
    z = np.sum(p, axis=1, keepdims=True)
    w1q = mxq(f64(w1), 0, "e4m3")
    tabidxg = tabu[:, idx]
    zh = w1q.T @ tabidxg
    ht = np.exp(zh * f64(temper))
    mz = ht.reshape(R, G, I // G).sum(axis=2)
    mzr = np.repeat(mz, I // G, axis=1)
    hv = ht / mzr * 4.0
    hs1 = hv * f64(hsc)
    goutq = mxq(f64(gout), 0, "e4m3")
    hs1q = mxq(hs1, 0, "e4m3")
    c0 = goutq.T @ hs1q
    dz = np.sum(c0 * p / np.square(z) * (-1.0), axis=1, keepdims=True)
    dp = c0 / z + dz
    da = dp * p
    gs = da * 512.0
    gf = np.zeros((Q, T))
    gf[:, idx] = gs
    y = f64(old) + gf
    return y

@@ -1,0 +1,183 @@
+from contextlib import ExitStack
+
+import concourse.mybir as mybir
+from concourse.masks import make_identity
+
+D, K, R, T, I, Q, G = 512, 512, 512, 2048, 512, 128, 64
+FLOPS = 2 * (D * Q * I + K * R * I + R * Q * I)
+
+F32 = mybir.dt.float32
+BF16 = mybir.dt.bfloat16
+I32 = mybir.dt.int32
+U32 = mybir.dt.uint32
+U16 = mybir.dt.uint16
+U8 = mybir.dt.uint8
+FP8X4 = mybir.dt.float8_e4m3fn_x4
+ALU = mybir.AluOpType
+ACT = mybir.ActivationFunctionType
+AX = mybir.AxisListType
+
+P = 128
+PACK = 4
+GROUP = I // G
+HALVES = 2
+HS = I // HALVES
+HG = G // HALVES
+STORE_EDGES = [0, 256, 768, 1408, 2048]
+
+
+def tile_attend_blrshared_soft_kernel(tc, query, keys_words, keys_scales, tab_words, tab_scales, w1, temper, gout, hsc, old, offs, out):
+    nc = tc.nc
+    with ExitStack() as ctx:
+        lists = ctx.enter_context(tc.tile_pool(name="lists", bufs=1))
+        sb = ctx.enter_context(tc.tile_pool(name="sb", bufs=1))
+        ps = ctx.enter_context(tc.psum_pool(name="ps", bufs=1))
+
+        def scale_pool(name, src, clearer, queue):
+            plane = sb.tile([P, T], U8, name=name, align_bytes=64)
+            clearer.memset(plane[:].bitcast(I32), 0)
+            for quad in range(4):
+                queue.dma_start(out=plane[32 * quad : 32 * quad + 4, :].bitcast(I32), in_=src[0, 4 * quad : 4 * quad + 4, :].bitcast(I32))
+            return plane
+
+        def word_pool(name, src):
+            words = sb.tile([P, T], U32, name=name, tag=name, align_bytes=64)
+            nc.sync.dma_start(out=words[:].bitcast(I32), in_=src[0].rearrange("p n t -> p (n t)").bitcast(I32))
+            return words
+
+        def quantise(name, grouped, width):
+            codes = sb.tile([P, width], U32, name=name + "_codes", align_bytes=64)
+            scales = sb.tile([P, width], U8, name=name + "_scales", align_bytes=64)
+            nc.vector.quantize_mx(out=codes[:].bitcast(FP8X4), scales=scales[:], in_=grouped)
+            return codes, scales
+
+        offsets = lists.tile([P, I // 16], U16, name="offsets")
+        tab_plane = scale_pool("tab_plane", tab_scales, nc.vector, nc.scalar)
+        keys_plane = scale_pool("keys_plane", keys_scales, nc.gpsimd, nc.gpsimd)
+        nc.sync.dma_start(offsets[:], offs)
+        temper_sb = sb.tile([P, PACK], F32, name="temper_sb")
+        nc.sync.dma_start(out=temper_sb[:], in_=temper.rearrange("(p t) o -> p (t o)", t=PACK))
+        hsc_sb = sb.tile([P, PACK], F32, name="hsc_sb")
+        nc.sync.dma_start(out=hsc_sb[:], in_=hsc.rearrange("(p t) o -> p (t o)", t=PACK))
+        w1_raw = sb.tile([P, PACK, R], F32, name="w1_raw")
+        nc.sync.dma_start(out=w1_raw[:], in_=w1.rearrange("(p j) r -> p j r", j=PACK))
+        tab_pool = word_pool("tab_pool", tab_words)
+        q_raw = sb.tile([P, PACK, Q], F32, name="q_raw", tag="small")
+        nc.sync.dma_start(out=q_raw[:], in_=query.rearrange("(p j) q -> p j q", j=PACK))
+        keys_pool = word_pool("keys_pool", keys_words)
+        ident = sb.tile([P, P], F32, name="ident")
+        make_identity(nc, ident[:])
+        placed = sb.tile([P, T], F32, name="placed")
+        nc.vector.memset(placed[:], 0.0)
+
+        w1_view = w1_raw[:].rearrange("p j (m t) -> p m t j", t=PACK)
+        w1_q = []
+        for pair, eng in enumerate((nc.scalar.copy, nc.vector.tensor_copy)):
+            grouped = sb.tile([P, 2, P, PACK], BF16, name="w1_grouped%d" % pair, align_bytes=64)
+            eng(out=grouped[:].rearrange("p t m j -> p m t j"), in_=w1_view[:, :, 2 * pair : 2 * pair + 2, :])
+            w1_q.append(quantise("w1_%d" % pair, grouped[:].rearrange("p t m j -> p (t m j)"), 2 * P))
+
+        tab_sc = sb.tile([P, I], U8, name="tab_sc", align_bytes=64)
+        nc.vector.tensor_copy(tab_sc[:], tab_plane[:].indirect(offsets[:]))
+
+        hsc4 = sb.tile([P, PACK], F32, name="hsc4")
+        nc.scalar.activation(out=hsc4[:], in_=hsc_sb[:], func=ACT.Copy, scale=4.0)
+
+        zh = [ps.tile([P, I], F32, name="zh%d" % t) for t in range(PACK)]
+        ht = []
+        for h in range(HALVES):
+            tab_w = sb.tile([P, HS], U32, name="tab_w%d" % h, align_bytes=64)
+            nc.vector.tensor_copy(tab_w[:], tab_pool[:].indirect(offsets[:, h * HS // 16 : (h + 1) * HS // 16]))
+            e = sb.tile([P, GROUP, PACK, HG], F32, name="ht%d" % h)
+            for t in range(PACK):
+                codes, scales = w1_q[t // 2]
+                cols = slice((t % 2) * P, (t % 2 + 1) * P)
+                nc.tensor.matmul_mx(out=zh[t][:, h * HS : (h + 1) * HS], lhsT=codes[:, cols].bitcast(FP8X4), lhsT_scale=scales[:, cols],
+                                    rhs=tab_w[:].bitcast(FP8X4), rhs_scale=tab_sc[:, h * HS : (h + 1) * HS], start=True, stop=True)
+                nc.scalar.activation(out=e[:, :, t, :], in_=zh[t][:, h * HS : (h + 1) * HS].rearrange("p (g j) -> p j g", j=GROUP),
+                                     func=ACT.Exp, scale=temper_sb[:, t : t + 1])
+            ht.append(e)
+
+        def interleave(name, raw):
+            grouped = sb.tile([P, Q, PACK], BF16, name=name, align_bytes=64)
+            nc.scalar.copy(out=grouped[:].rearrange("p (c i) j -> p c j i", i=4), in_=raw[:].rearrange("p j (c i) -> p c j i", i=4))
+            return grouped[:].rearrange("p q j -> p (q j)")
+
+        q_codes, q_scales = quantise("q", interleave("q_grouped", q_raw), Q)
+        g_raw = sb.tile([P, PACK, Q], F32, name="g_raw", tag="small")
+        nc.sync.dma_start(out=g_raw[:], in_=gout.rearrange("(p j) q -> p j q", j=PACK))
+
+        keys_sc = sb.tile([P, I], U8, name="keys_sc", align_bytes=64)
+        nc.vector.tensor_copy(keys_sc[:], keys_plane[:].indirect(offsets[:]))
+        keys_w = sb.tile([P, I], U32, name="keys_w", align_bytes=64)
+        nc.vector.tensor_copy(keys_w[:], keys_pool[:].indirect(offsets[:]))
+
+        old_sb = sb.tile([P, T], F32, name="old_sb", tag="keys_pool", align_bytes=64)
+        nc.sync.dma_start(out=old_sb[:], in_=old)
+
+        sums = []
+        for h in range(HALVES):
+            bank = ps.tile([P, 2, P], F32, name="sums%d" % h)
+            for j in range(GROUP):
+                nc.tensor.matmul(out=bank[:, 0, :], lhsT=ht[h][:, j, :, :].rearrange("p t g -> p (t g)"), rhs=ident[:],
+                                 is_transpose=True, start=(j == 0), stop=(j == GROUP - 1))
+            sums.append(bank)
+
+        a = ps.tile([P, I], F32, name="a")
+        nc.tensor.matmul_mx(out=a[:], lhsT=q_codes[:].bitcast(FP8X4), lhsT_scale=q_scales[:], rhs=keys_w[:].bitcast(FP8X4), rhs_scale=keys_sc[:], start=True, stop=True)
+
+        hts = []
+        for h in range(HALVES):
+            rec_t = sb.tile([P, P], F32, name="rec_t%d" % h)
+            nc.vector.reciprocal(out=rec_t[:], in_=sums[h][:, 0, :])
+            nc.tensor.transpose(sums[h][:, 1, :], rec_t[:], ident[:])
+            s = sb.tile([P, GROUP, PACK, HG], F32, name="hts%d" % h)
+            for t in range(PACK):
+                nc.scalar.activation(out=s[:, :, t, :], in_=ht[h][:, :, t, :], func=ACT.Copy, scale=hsc4[:, t : t + 1])
+            hts.append(s)
+
+        nmax = sb.tile([P, 1], F32, name="nmax")
+        nc.vector.tensor_reduce(out=nmax[:], in_=a[:], axis=AX.X, op=ALU.max, negate=True)
+        p = sb.tile([P, I], F32, name="p")
+        z = sb.tile([P, 1], F32, name="z")
+        nc.scalar.activation(out=p[:], in_=a[:], func=ACT.Exp, bias=nmax[:], scale=1.0, accum_out=z[:])
+        g_codes, g_scales = quantise("g", interleave("g_grouped", g_raw), Q)
+
+        rz = sb.tile([P, 1], F32, name="rz")
+        nc.vector.reciprocal(out=rz[:], in_=z[:])
+        rz512 = sb.tile([P, 1], F32, name="rz512")
+        nc.scalar.activation(out=rz512[:], in_=rz[:], func=ACT.Copy, scale=512.0)
+        pa = sb.tile([P, I], F32, name="pa")
+        nc.scalar.activation(out=pa[:], in_=p[:], func=ACT.Copy, scale=rz512[:])
+
+        hs = []
+        for h in range(HALVES):
+            grouped = sb.tile([P, GROUP, HG, PACK], BF16, name="hs%d" % h, align_bytes=64)
+            rec = sums[h][:, 1, :].rearrange("p (t g) -> p g t", t=PACK).unsqueeze(1).to_broadcast([P, GROUP, HG, PACK])
+            nc.vector.tensor_tensor(out=grouped[:], in0=hts[h][:].rearrange("p j t g -> p j g t"), in1=rec, op=ALU.mult)
+            hs.append(grouped)
+
+        c0 = []
+        shift = []
+        for h in range(HALVES):
+            codes, scales = quantise("hs%d" % h, hs[h][:].rearrange("p j g t -> p (j g t)"), HS)
+            bank = ps.tile([P, HS], F32, name="c0_%d" % h, tag=("c0", "zh0")[h])
+            nc.tensor.matmul_mx(out=bank[:], lhsT=g_codes[:].bitcast(FP8X4), lhsT_scale=g_scales[:], rhs=codes[:].bitcast(FP8X4), rhs_scale=scales[:], start=True, stop=True)
+            by_slot = bank[:].rearrange("p (j g) -> p g j", j=GROUP)
+            prod = sb.tile([P, HG, GROUP], F32, name="prod%d" % h)
+            part = sb.tile([P, 1], F32, name="part%d" % h)
+            nc.vector.scalar_tensor_tensor(out=prod[:], in0=by_slot, scalar=-1.0 / 512.0, in1=pa[:, h * HS : (h + 1) * HS].rearrange("p (g j) -> p g j", j=GROUP),
+                                           op0=ALU.mult, op1=ALU.mult, accum_out=part[:])
+            c0.append(by_slot)
+            shift.append(part)
+
+        d = sb.tile([P, I], F32, name="d")
+        for h in range(HALVES):
+            nc.vector.tensor_scalar(out=d[:, h * HS : (h + 1) * HS].rearrange("p (g j) -> p g j", j=GROUP), in0=c0[h], scalar1=shift[0][:], scalar2=shift[1][:], op0=ALU.add, op1=ALU.add)
+        nc.vector.tensor_tensor(placed[:].indirect(offsets[:]), d[:], pa[:], ALU.mult)
+
+        for c in range(len(STORE_EDGES) - 1):
+            cols = slice(STORE_EDGES[c], STORE_EDGES[c + 1])
+            res = sb.tile([P, STORE_EDGES[c + 1] - STORE_EDGES[c]], F32, name="res%d" % c)
+            nc.vector.tensor_tensor(out=res[:], in0=placed[:, cols], in1=old_sb[:, cols], op=ALU.add)
+            nc.sync.dma_start(out=out[:, cols], in_=res[:])

@@ -23,7 +23,7 @@ GROUP = I // G
 HALVES = 2
 HS = I // HALVES
 HG = G // HALVES
-STORE_EDGES = [0, 256, 768, 1408, 2048]
+STORE_EDGES = [0, 512, 1024, 1536, 2048]
 
 
 def tile_attend_blrshared_soft_kernel(tc, query, keys_words, keys_scales, tab_words, tab_scales, w1, temper, gout, hsc, old, offs, out):
@@ -33,15 +33,15 @@ def tile_attend_blrshared_soft_kernel(tc, query, keys_words, keys_scales, tab_wo
         sb = ctx.enter_context(tc.tile_pool(name="sb", bufs=1))
         ps = ctx.enter_context(tc.psum_pool(name="ps", bufs=1))
 
-        def scale_pool(name, src, clearer, queue):
-            plane = sb.tile([P, T], U8, name=name, align_bytes=64)
-            clearer.memset(plane[:].bitcast(I32), 0)
+        def scale_pool(name, src, tag):
+            plane = sb.tile([P, T], U8, name=name, tag=tag, align_bytes=64)
+            nc.vector.memset(plane[:].bitcast(I32), 0)
             for quad in range(4):
-                queue.dma_start(out=plane[32 * quad : 32 * quad + 4, :].bitcast(I32), in_=src[0, 4 * quad : 4 * quad + 4, :].bitcast(I32))
+                nc.scalar.dma_start(out=plane[32 * quad : 32 * quad + 4, :].bitcast(I32), in_=src[0, 4 * quad : 4 * quad + 4, :].bitcast(I32))
             return plane
 
-        def word_pool(name, src):
-            words = sb.tile([P, T], U32, name=name, tag=name, align_bytes=64)
+        def word_pool(name, src, tag):
+            words = sb.tile([P, T], U32, name=name, tag=tag, align_bytes=64)
             nc.sync.dma_start(out=words[:].bitcast(I32), in_=src[0].rearrange("p n t -> p (n t)").bitcast(I32))
             return words
 
@@ -52,19 +52,17 @@ def tile_attend_blrshared_soft_kernel(tc, query, keys_words, keys_scales, tab_wo
             return codes, scales
 
         offsets = lists.tile([P, I // 16], U16, name="offsets")
-        tab_plane = scale_pool("tab_plane", tab_scales, nc.vector, nc.scalar)
-        keys_plane = scale_pool("keys_plane", keys_scales, nc.gpsimd, nc.gpsimd)
+        tab_plane = scale_pool("tab_plane", tab_scales, "tab_plane")
         nc.sync.dma_start(offsets[:], offs)
         temper_sb = sb.tile([P, PACK], F32, name="temper_sb")
         nc.sync.dma_start(out=temper_sb[:], in_=temper.rearrange("(p t) o -> p (t o)", t=PACK))
         hsc_sb = sb.tile([P, PACK], F32, name="hsc_sb")
         nc.sync.dma_start(out=hsc_sb[:], in_=hsc.rearrange("(p t) o -> p (t o)", t=PACK))
-        w1_raw = sb.tile([P, PACK, R], F32, name="w1_raw")
+        w1_raw = sb.tile([P, PACK, R], F32, name="w1_raw", tag="w1_then_keys", align_bytes=64)
         nc.sync.dma_start(out=w1_raw[:], in_=w1.rearrange("(p j) r -> p j r", j=PACK))
-        tab_pool = word_pool("tab_pool", tab_words)
-        q_raw = sb.tile([P, PACK, Q], F32, name="q_raw", tag="small")
+        tab_pool = word_pool("tab_pool", tab_words, "tab_pool")
+        q_raw = sb.tile([P, PACK, Q], F32, name="q_raw", tag="rows")
         nc.sync.dma_start(out=q_raw[:], in_=query.rearrange("(p j) q -> p j q", j=PACK))
-        keys_pool = word_pool("keys_pool", keys_words)
         ident = sb.tile([P, P], F32, name="ident")
         make_identity(nc, ident[:])
         placed = sb.tile([P, T], F32, name="placed")
@@ -73,12 +71,13 @@ def tile_attend_blrshared_soft_kernel(tc, query, keys_words, keys_scales, tab_wo
         w1_view = w1_raw[:].rearrange("p j (m t) -> p m t j", t=PACK)
         w1_q = []
         for pair, eng in enumerate((nc.scalar.copy, nc.vector.tensor_copy)):
-            grouped = sb.tile([P, 2, P, PACK], BF16, name="w1_grouped%d" % pair, align_bytes=64)
+            grouped = sb.tile([P, 2, P, PACK], BF16, name="w1_grouped%d" % pair, tag="w1_grouped%d" % pair, align_bytes=64)
             eng(out=grouped[:].rearrange("p t m j -> p m t j"), in_=w1_view[:, :, 2 * pair : 2 * pair + 2, :])
             w1_q.append(quantise("w1_%d" % pair, grouped[:].rearrange("p t m j -> p (t m j)"), 2 * P))
 
-        tab_sc = sb.tile([P, I], U8, name="tab_sc", align_bytes=64)
-        nc.vector.tensor_copy(tab_sc[:], tab_plane[:].indirect(offsets[:]))
+
+        keys_pool = word_pool("keys_pool", keys_words, "w1_then_keys")
+        keys_plane = scale_pool("keys_plane", keys_scales, "w1_grouped1")
 
         hsc4 = sb.tile([P, PACK], F32, name="hsc4")
         nc.scalar.activation(out=hsc4[:], in_=hsc_sb[:], func=ACT.Copy, scale=4.0)
@@ -86,14 +85,17 @@ def tile_attend_blrshared_soft_kernel(tc, query, keys_words, keys_scales, tab_wo
         zh = [ps.tile([P, I], F32, name="zh%d" % t) for t in range(PACK)]
         ht = []
         for h in range(HALVES):
+            picks = offsets[:, h * HS // 16 : (h + 1) * HS // 16]
+            tab_sc = sb.tile([P, HS], U8, name="tab_sc%d" % h, align_bytes=64)
+            nc.vector.tensor_copy(tab_sc[:], tab_plane[:].indirect(picks))
             tab_w = sb.tile([P, HS], U32, name="tab_w%d" % h, align_bytes=64)
-            nc.vector.tensor_copy(tab_w[:], tab_pool[:].indirect(offsets[:, h * HS // 16 : (h + 1) * HS // 16]))
+            nc.vector.tensor_copy(tab_w[:], tab_pool[:].indirect(picks))
             e = sb.tile([P, GROUP, PACK, HG], F32, name="ht%d" % h)
             for t in range(PACK):
                 codes, scales = w1_q[t // 2]
                 cols = slice((t % 2) * P, (t % 2 + 1) * P)
                 nc.tensor.matmul_mx(out=zh[t][:, h * HS : (h + 1) * HS], lhsT=codes[:, cols].bitcast(FP8X4), lhsT_scale=scales[:, cols],
-                                    rhs=tab_w[:].bitcast(FP8X4), rhs_scale=tab_sc[:, h * HS : (h + 1) * HS], start=True, stop=True)
+                                    rhs=tab_w[:].bitcast(FP8X4), rhs_scale=tab_sc[:], start=True, stop=True)
                 nc.scalar.activation(out=e[:, :, t, :], in_=zh[t][:, h * HS : (h + 1) * HS].rearrange("p (g j) -> p j g", j=GROUP),
                                      func=ACT.Exp, scale=temper_sb[:, t : t + 1])
             ht.append(e)
@@ -104,7 +106,7 @@ def tile_attend_blrshared_soft_kernel(tc, query, keys_words, keys_scales, tab_wo
             return grouped[:].rearrange("p q j -> p (q j)")
 
         q_codes, q_scales = quantise("q", interleave("q_grouped", q_raw), Q)
-        g_raw = sb.tile([P, PACK, Q], F32, name="g_raw", tag="small")
+        g_raw = sb.tile([P, PACK, Q], F32, name="g_raw", tag="rows")
         nc.sync.dma_start(out=g_raw[:], in_=gout.rearrange("(p j) q -> p j q", j=PACK))
 
         keys_sc = sb.tile([P, I], U8, name="keys_sc", align_bytes=64)
@@ -112,7 +114,7 @@ def tile_attend_blrshared_soft_kernel(tc, query, keys_words, keys_scales, tab_wo
         keys_w = sb.tile([P, I], U32, name="keys_w", align_bytes=64)
         nc.vector.tensor_copy(keys_w[:], keys_pool[:].indirect(offsets[:]))
 
-        old_sb = sb.tile([P, T], F32, name="old_sb", tag="keys_pool", align_bytes=64)
+        old_sb = sb.tile([P, T], F32, name="old_sb", tag="w1_then_keys", align_bytes=64)
         nc.sync.dma_start(out=old_sb[:], in_=old)
 
         sums = []

@@ -20,6 +20,7 @@ AX = mybir.AxisListType
 P = 128
 PACK = 4
 GROUP = I // G
+PAIRS = GROUP // 2
 HALVES = 2
 HS = I // HALVES
 HG = G // HALVES
@@ -33,11 +34,11 @@ def tile_attend_blrshared_soft_kernel(tc, query, keys_words, keys_scales, tab_wo
         sb = ctx.enter_context(tc.tile_pool(name="sb", bufs=1))
         ps = ctx.enter_context(tc.psum_pool(name="ps", bufs=1))
 
-        def scale_pool(name, src, tag):
+        def scale_pool(name, src, tag, clearer, queue):
             plane = sb.tile([P, T], U8, name=name, tag=tag, align_bytes=64)
-            nc.vector.memset(plane[:].bitcast(I32), 0)
+            clearer.memset(plane[:].bitcast(I32), 0)
             for quad in range(4):
-                nc.scalar.dma_start(out=plane[32 * quad : 32 * quad + 4, :].bitcast(I32), in_=src[0, 4 * quad : 4 * quad + 4, :].bitcast(I32))
+                queue.dma_start(out=plane[32 * quad : 32 * quad + 4, :].bitcast(I32), in_=src[0, 4 * quad : 4 * quad + 4, :].bitcast(I32))
             return plane
 
         def word_pool(name, src, tag):
@@ -52,35 +53,35 @@ def tile_attend_blrshared_soft_kernel(tc, query, keys_words, keys_scales, tab_wo
             return codes, scales
 
         offsets = lists.tile([P, I // 16], U16, name="offsets")
-        tab_plane = scale_pool("tab_plane", tab_scales, "tab_plane")
+        tab_plane = scale_pool("tab_plane", tab_scales, "tab_plane", nc.gpsimd, nc.sync)
         nc.sync.dma_start(offsets[:], offs)
+        w1_raw = sb.tile([P, PACK, R], F32, name="w1_raw")
+        nc.sync.dma_start(out=w1_raw[:], in_=w1.rearrange("(p j) r -> p j r", j=PACK))
         temper_sb = sb.tile([P, PACK], F32, name="temper_sb")
         nc.sync.dma_start(out=temper_sb[:], in_=temper.rearrange("(p t) o -> p (t o)", t=PACK))
-        hsc_sb = sb.tile([P, PACK], F32, name="hsc_sb")
+        hsc_sb = sb.tile([P, PACK], F32, name="hsc_sb", tag="hsc_keys_old", align_bytes=64)
         nc.sync.dma_start(out=hsc_sb[:], in_=hsc.rearrange("(p t) o -> p (t o)", t=PACK))
-        w1_raw = sb.tile([P, PACK, R], F32, name="w1_raw", tag="w1_then_keys", align_bytes=64)
-        nc.sync.dma_start(out=w1_raw[:], in_=w1.rearrange("(p j) r -> p j r", j=PACK))
         tab_pool = word_pool("tab_pool", tab_words, "tab_pool")
-        q_raw = sb.tile([P, PACK, Q], F32, name="q_raw", tag="rows")
+        q_raw = sb.tile([P, PACK, Q], F32, name="q_raw")
         nc.sync.dma_start(out=q_raw[:], in_=query.rearrange("(p j) q -> p j q", j=PACK))
+        keys_plane = scale_pool("keys_plane", keys_scales, "keys_plane", nc.vector, nc.sync)
+        hsc4 = sb.tile([P, PACK], F32, name="hsc4")
+        nc.scalar.activation(out=hsc4[:], in_=hsc_sb[:], func=ACT.Copy, scale=4.0)
+        keys_pool = word_pool("keys_pool", keys_words, "hsc_keys_old")
         ident = sb.tile([P, P], F32, name="ident")
         make_identity(nc, ident[:])
         placed = sb.tile([P, T], F32, name="placed")
         nc.vector.memset(placed[:], 0.0)
 
-        w1_view = w1_raw[:].rearrange("p j (m t) -> p m t j", t=PACK)
+        w1_view = w1_raw[:].rearrange("p j (m t) -> p m j t", t=PACK)
         w1_q = []
         for pair, eng in enumerate((nc.scalar.copy, nc.vector.tensor_copy)):
             grouped = sb.tile([P, 2, P, PACK], BF16, name="w1_grouped%d" % pair, tag="w1_grouped%d" % pair, align_bytes=64)
-            eng(out=grouped[:].rearrange("p t m j -> p m t j"), in_=w1_view[:, :, 2 * pair : 2 * pair + 2, :])
+            eng(out=grouped[:].rearrange("p t m j -> p m j t"), in_=w1_view[:, :, :, 2 * pair : 2 * pair + 2])
             w1_q.append(quantise("w1_%d" % pair, grouped[:].rearrange("p t m j -> p (t m j)"), 2 * P))
 
-
-        keys_pool = word_pool("keys_pool", keys_words, "w1_then_keys")
-        keys_plane = scale_pool("keys_plane", keys_scales, "w1_grouped1")
-
-        hsc4 = sb.tile([P, PACK], F32, name="hsc4")
-        nc.scalar.activation(out=hsc4[:], in_=hsc_sb[:], func=ACT.Copy, scale=4.0)
+        g_raw = sb.tile([P, PACK, Q], F32, name="g_raw", tag="w1_grouped0", align_bytes=64)
+        nc.sync.dma_start(out=g_raw[:], in_=gout.rearrange("(p j) q -> p j q", j=PACK))
 
         zh = [ps.tile([P, I], F32, name="zh%d" % t) for t in range(PACK)]
         ht = []
@@ -90,38 +91,33 @@ def tile_attend_blrshared_soft_kernel(tc, query, keys_words, keys_scales, tab_wo
             nc.vector.tensor_copy(tab_sc[:], tab_plane[:].indirect(picks))
             tab_w = sb.tile([P, HS], U32, name="tab_w%d" % h, align_bytes=64)
             nc.vector.tensor_copy(tab_w[:], tab_pool[:].indirect(picks))
-            e = sb.tile([P, GROUP, PACK, HG], F32, name="ht%d" % h)
+            e = sb.tile([P, PAIRS, PACK, HG, 2], F32, name="ht%d" % h)
             for t in range(PACK):
                 codes, scales = w1_q[t // 2]
                 cols = slice((t % 2) * P, (t % 2 + 1) * P)
                 nc.tensor.matmul_mx(out=zh[t][:, h * HS : (h + 1) * HS], lhsT=codes[:, cols].bitcast(FP8X4), lhsT_scale=scales[:, cols],
                                     rhs=tab_w[:].bitcast(FP8X4), rhs_scale=tab_sc[:], start=True, stop=True)
-                nc.scalar.activation(out=e[:, :, t, :], in_=zh[t][:, h * HS : (h + 1) * HS].rearrange("p (g j) -> p j g", j=GROUP),
+                nc.scalar.activation(out=e[:, :, t, :, :], in_=zh[t][:, h * HS : (h + 1) * HS].rearrange("p (g u e) -> p u g e", u=PAIRS, e=2),
                                      func=ACT.Exp, scale=temper_sb[:, t : t + 1])
             ht.append(e)
 
-        def interleave(name, raw):
+        def interleave(name, raw, copy):
             grouped = sb.tile([P, Q, PACK], BF16, name=name, align_bytes=64)
-            nc.scalar.copy(out=grouped[:].rearrange("p (c i) j -> p c j i", i=4), in_=raw[:].rearrange("p j (c i) -> p c j i", i=4))
+            copy(out=grouped[:].rearrange("p (c i) j -> p c j i", i=4), in_=raw[:].rearrange("p j (c i) -> p c j i", i=4))
             return grouped[:].rearrange("p q j -> p (q j)")
 
-        q_codes, q_scales = quantise("q", interleave("q_grouped", q_raw), Q)
-        g_raw = sb.tile([P, PACK, Q], F32, name="g_raw", tag="rows")
-        nc.sync.dma_start(out=g_raw[:], in_=gout.rearrange("(p j) q -> p j q", j=PACK))
+        q_codes, q_scales = quantise("q", interleave("q_grouped", q_raw, nc.vector.tensor_copy), Q)
 
-        keys_sc = sb.tile([P, I], U8, name="keys_sc", align_bytes=64)
+        keys_sc = sb.tile([P, I], U8, name="keys_sc", tag="tab_pool", align_bytes=64)
         nc.vector.tensor_copy(keys_sc[:], keys_plane[:].indirect(offsets[:]))
         keys_w = sb.tile([P, I], U32, name="keys_w", align_bytes=64)
         nc.vector.tensor_copy(keys_w[:], keys_pool[:].indirect(offsets[:]))
-
-        old_sb = sb.tile([P, T], F32, name="old_sb", tag="w1_then_keys", align_bytes=64)
-        nc.sync.dma_start(out=old_sb[:], in_=old)
 
         sums = []
         for h in range(HALVES):
             bank = ps.tile([P, 2, P], F32, name="sums%d" % h)
             for j in range(GROUP):
-                nc.tensor.matmul(out=bank[:, 0, :], lhsT=ht[h][:, j, :, :].rearrange("p t g -> p (t g)"), rhs=ident[:],
+                nc.tensor.matmul(out=bank[:, 0, :], lhsT=ht[h][:, j // 2, :, :, j % 2].rearrange("p t g -> p (t g)"), rhs=ident[:],
                                  is_transpose=True, start=(j == 0), stop=(j == GROUP - 1))
             sums.append(bank)
 
@@ -130,52 +126,61 @@ def tile_attend_blrshared_soft_kernel(tc, query, keys_words, keys_scales, tab_wo
 
         hts = []
         for h in range(HALVES):
-            rec_t = sb.tile([P, P], F32, name="rec_t%d" % h)
+            rec_t = sb.tile([P, P], F32, name="rec_t%d" % h, tag="hsc_keys_old", align_bytes=64)
             nc.vector.reciprocal(out=rec_t[:], in_=sums[h][:, 0, :])
             nc.tensor.transpose(sums[h][:, 1, :], rec_t[:], ident[:])
-            s = sb.tile([P, GROUP, PACK, HG], F32, name="hts%d" % h)
+            s = sb.tile([P, PAIRS, PACK, HG, 2], F32, name="hts%d" % h)
             for t in range(PACK):
-                nc.scalar.activation(out=s[:, :, t, :], in_=ht[h][:, :, t, :], func=ACT.Copy, scale=hsc4[:, t : t + 1])
+                nc.scalar.activation(out=s[:, :, t, :, :], in_=ht[h][:, :, t, :, :], func=ACT.Copy, scale=hsc4[:, t : t + 1])
             hts.append(s)
+            if h == 0:
+                nmax = sb.tile([P, 1], F32, name="nmax")
+                nc.vector.tensor_reduce(out=nmax[:], in_=a[:], axis=AX.X, op=ALU.max, negate=True)
+                p = sb.tile([P, I], F32, name="p")
+                z = sb.tile([P, 1], F32, name="z")
+                nc.scalar.activation(out=p[:], in_=a[:], func=ACT.Exp, bias=nmax[:], scale=1.0, accum_out=z[:])
 
-        nmax = sb.tile([P, 1], F32, name="nmax")
-        nc.vector.tensor_reduce(out=nmax[:], in_=a[:], axis=AX.X, op=ALU.max, negate=True)
-        p = sb.tile([P, I], F32, name="p")
-        z = sb.tile([P, 1], F32, name="z")
-        nc.scalar.activation(out=p[:], in_=a[:], func=ACT.Exp, bias=nmax[:], scale=1.0, accum_out=z[:])
-        g_codes, g_scales = quantise("g", interleave("g_grouped", g_raw), Q)
+        old_sb = sb.tile([P, T], F32, name="old_sb", tag="hsc_keys_old", align_bytes=64)
+        nc.sync.dma_start(out=old_sb[:], in_=old)
+
+        g_codes, g_scales = quantise("g", interleave("g_grouped", g_raw, nc.scalar.copy), Q)
 
         rz = sb.tile([P, 1], F32, name="rz")
         nc.vector.reciprocal(out=rz[:], in_=z[:])
         rz512 = sb.tile([P, 1], F32, name="rz512")
         nc.scalar.activation(out=rz512[:], in_=rz[:], func=ACT.Copy, scale=512.0)
+
+        p_dealt = sb.tile([P, PAIRS, HG, 2], F32, name="p_dealt")
+        nc.scalar.copy(out=p_dealt[:], in_=p[:, HS:].rearrange("p (g u e) -> p u g e", u=PAIRS, e=2))
         pa = sb.tile([P, I], F32, name="pa")
         nc.scalar.activation(out=pa[:], in_=p[:], func=ACT.Copy, scale=rz512[:])
 
         hs = []
         for h in range(HALVES):
-            grouped = sb.tile([P, GROUP, HG, PACK], BF16, name="hs%d" % h, align_bytes=64)
-            rec = sums[h][:, 1, :].rearrange("p (t g) -> p g t", t=PACK).unsqueeze(1).to_broadcast([P, GROUP, HG, PACK])
-            nc.vector.tensor_tensor(out=grouped[:], in0=hts[h][:].rearrange("p j t g -> p j g t"), in1=rec, op=ALU.mult)
+            grouped = sb.tile([P, PAIRS, HG, 2, PACK], BF16, name="hs%d" % h, align_bytes=64)
+            rec = sums[h][:, 1, :].rearrange("p (t g) -> p g t", t=PACK).unsqueeze(3).to_broadcast([P, HG, PACK, 2])
+            for u in range(PAIRS):
+                nc.vector.tensor_tensor(out=grouped[:, u].rearrange("p g e t -> p g t e"), in0=hts[h][:, u].rearrange("p t g e -> p g t e"), in1=rec, op=ALU.mult)
             hs.append(grouped)
 
         c0 = []
-        shift = []
         for h in range(HALVES):
-            codes, scales = quantise("hs%d" % h, hs[h][:].rearrange("p j g t -> p (j g t)"), HS)
+            codes, scales = quantise("hs%d" % h, hs[h][:].rearrange("p u g e t -> p (u g e t)"), HS)
             bank = ps.tile([P, HS], F32, name="c0_%d" % h, tag=("c0", "zh0")[h])
             nc.tensor.matmul_mx(out=bank[:], lhsT=g_codes[:].bitcast(FP8X4), lhsT_scale=g_scales[:], rhs=codes[:].bitcast(FP8X4), rhs_scale=scales[:], start=True, stop=True)
-            by_slot = bank[:].rearrange("p (j g) -> p g j", j=GROUP)
-            prod = sb.tile([P, HG, GROUP], F32, name="prod%d" % h)
+            c0.append(bank)
+        by_slot = [bank[:].rearrange("p (u g e) -> p g u e", u=PAIRS, e=2) for bank in c0]
+        c0_first = sb.tile([P, HS], F32, name="c0_first")
+        nc.scalar.copy(out=c0_first[:].rearrange("p (g u e) -> p g u e", u=PAIRS, e=2), in_=by_slot[0])
+        prod = sb.tile([P, HALVES, HS], F32, name="prod")
+        shift = []
+        for h, (values, weights) in enumerate(((c0_first[:], p[:, :HS]), (c0[1][:], p_dealt[:].rearrange("p u g e -> p (u g e)")))):
             part = sb.tile([P, 1], F32, name="part%d" % h)
-            nc.vector.scalar_tensor_tensor(out=prod[:], in0=by_slot, scalar=-1.0 / 512.0, in1=pa[:, h * HS : (h + 1) * HS].rearrange("p (g j) -> p g j", j=GROUP),
-                                           op0=ALU.mult, op1=ALU.mult, accum_out=part[:])
-            c0.append(by_slot)
+            nc.vector.scalar_tensor_tensor(out=prod[:, h, :], in0=values, scalar=rz[:], in1=weights, op0=ALU.mult, op1=ALU.mult, accum_out=part[:])
             shift.append(part)
-
         d = sb.tile([P, I], F32, name="d")
-        for h in range(HALVES):
-            nc.vector.tensor_scalar(out=d[:, h * HS : (h + 1) * HS].rearrange("p (g j) -> p g j", j=GROUP), in0=c0[h], scalar1=shift[0][:], scalar2=shift[1][:], op0=ALU.add, op1=ALU.add)
+        nc.vector.tensor_scalar(out=d[:, :HS], in0=c0_first[:], scalar1=shift[0][:], scalar2=shift[1][:], op0=ALU.subtract, op1=ALU.subtract)
+        nc.vector.tensor_scalar(out=d[:, HS:].rearrange("p (g u e) -> p g u e", u=PAIRS, e=2), in0=by_slot[1], scalar1=shift[0][:], scalar2=shift[1][:], op0=ALU.subtract, op1=ALU.subtract)
         nc.vector.tensor_tensor(placed[:].indirect(offsets[:]), d[:], pa[:], ALU.mult)
 
         for c in range(len(STORE_EDGES) - 1):

@@ -91,13 +91,13 @@ def tile_attend_blrshared_soft_kernel(tc, query, keys_words, keys_scales, tab_wo
             nc.vector.tensor_copy(tab_sc[:], tab_plane[:].indirect(picks))
             tab_w = sb.tile([P, HS], U32, name="tab_w%d" % h, align_bytes=64)
             nc.vector.tensor_copy(tab_w[:], tab_pool[:].indirect(picks))
-            e = sb.tile([P, PAIRS, PACK, HG, 2], F32, name="ht%d" % h)
+            e = sb.tile([P, GROUP, PACK, HG], F32, name="ht%d" % h)
             for t in range(PACK):
                 codes, scales = w1_q[t // 2]
                 cols = slice((t % 2) * P, (t % 2 + 1) * P)
                 nc.tensor.matmul_mx(out=zh[t][:, h * HS : (h + 1) * HS], lhsT=codes[:, cols].bitcast(FP8X4), lhsT_scale=scales[:, cols],
                                     rhs=tab_w[:].bitcast(FP8X4), rhs_scale=tab_sc[:], start=True, stop=True)
-                nc.scalar.activation(out=e[:, :, t, :, :], in_=zh[t][:, h * HS : (h + 1) * HS].rearrange("p (g u e) -> p u g e", u=PAIRS, e=2),
+                nc.scalar.activation(out=e[:, :, t, :], in_=zh[t][:, h * HS : (h + 1) * HS].rearrange("p (g j) -> p j g", j=GROUP),
                                      func=ACT.Exp, scale=temper_sb[:, t : t + 1])
             ht.append(e)
 
@@ -117,7 +117,7 @@ def tile_attend_blrshared_soft_kernel(tc, query, keys_words, keys_scales, tab_wo
         for h in range(HALVES):
             bank = ps.tile([P, 2, P], F32, name="sums%d" % h)
             for j in range(GROUP):
-                nc.tensor.matmul(out=bank[:, 0, :], lhsT=ht[h][:, j // 2, :, :, j % 2].rearrange("p t g -> p (t g)"), rhs=ident[:],
+                nc.tensor.matmul(out=bank[:, 0, :], lhsT=ht[h][:, j, :, :].rearrange("p t g -> p (t g)"), rhs=ident[:],
                                  is_transpose=True, start=(j == 0), stop=(j == GROUP - 1))
             sums.append(bank)
 
@@ -131,7 +131,7 @@ def tile_attend_blrshared_soft_kernel(tc, query, keys_words, keys_scales, tab_wo
             nc.tensor.transpose(sums[h][:, 1, :], rec_t[:], ident[:])
             s = sb.tile([P, PAIRS, PACK, HG, 2], F32, name="hts%d" % h)
             for t in range(PACK):
-                nc.scalar.activation(out=s[:, :, t, :, :], in_=ht[h][:, :, t, :, :], func=ACT.Copy, scale=hsc4[:, t : t + 1])
+                nc.scalar.activation(out=s[:, :, t, :, :], in_=ht[h][:, :, t, :].rearrange("p (u e) g -> p u g e", e=2), func=ACT.Copy, scale=hsc4[:, t : t + 1])
             hts.append(s)
             if h == 0:
                 nmax = sb.tile([P, 1], F32, name="nmax")
@@ -155,24 +155,21 @@ def tile_attend_blrshared_soft_kernel(tc, query, keys_words, keys_scales, tab_wo
         pa = sb.tile([P, I], F32, name="pa")
         nc.scalar.activation(out=pa[:], in_=p[:], func=ACT.Copy, scale=rz512[:])
 
-        hs = []
+        c0 = []
         for h in range(HALVES):
-            grouped = sb.tile([P, PAIRS, HG, 2, PACK], BF16, name="hs%d" % h, align_bytes=64)
+            grouped = sb.tile([P, PAIRS, HG, 2, PACK], BF16, name="hs%d" % h, tag="hs%d" % h, align_bytes=64)
             rec = sums[h][:, 1, :].rearrange("p (t g) -> p g t", t=PACK).unsqueeze(3).to_broadcast([P, HG, PACK, 2])
             for u in range(PAIRS):
                 nc.vector.tensor_tensor(out=grouped[:, u].rearrange("p g e t -> p g t e"), in0=hts[h][:, u].rearrange("p t g e -> p g t e"), in1=rec, op=ALU.mult)
-            hs.append(grouped)
-
-        c0 = []
-        for h in range(HALVES):
-            codes, scales = quantise("hs%d" % h, hs[h][:].rearrange("p u g e t -> p (u g e t)"), HS)
+            codes, scales = quantise("hs%d" % h, grouped[:].rearrange("p u g e t -> p (u g e t)"), HS)
             bank = ps.tile([P, HS], F32, name="c0_%d" % h, tag=("c0", "zh0")[h])
             nc.tensor.matmul_mx(out=bank[:], lhsT=g_codes[:].bitcast(FP8X4), lhsT_scale=g_scales[:], rhs=codes[:].bitcast(FP8X4), rhs_scale=scales[:], start=True, stop=True)
             c0.append(bank)
+
         by_slot = [bank[:].rearrange("p (u g e) -> p g u e", u=PAIRS, e=2) for bank in c0]
         c0_first = sb.tile([P, HS], F32, name="c0_first")
         nc.scalar.copy(out=c0_first[:].rearrange("p (g u e) -> p g u e", u=PAIRS, e=2), in_=by_slot[0])
-        prod = sb.tile([P, HALVES, HS], F32, name="prod")
+        prod = sb.tile([P, HALVES, HS], F32, name="prod", tag="hs1", align_bytes=64)
         shift = []
         for h, (values, weights) in enumerate(((c0_first[:], p[:, :HS]), (c0[1][:], p_dealt[:].rearrange("p u g e -> p (u g e)")))):
             part = sb.tile([P, 1], F32, name="part%d" % h)

@@ -19,12 +19,15 @@ AX = mybir.AxisListType
 
 P = 128
 PACK = 4
+QUADRANT = 32
+LIST_COLUMN = 16
+ALIGN = 64
 GROUP = I // G
 PAIRS = GROUP // 2
 HALVES = 2
-HS = I // HALVES
-HG = G // HALVES
-STORE_EDGES = [0, 512, 1024, 1536, 2048]
+HALF_SLOTS = I // HALVES
+HALF_GROUPS = G // HALVES
+STORE_EDGES = [0, 256, 704, 1152, 1600, 2048]
 
 
 def tile_attend_blrshared_soft_kernel(tc, query, keys_words, keys_scales, tab_words, tab_scales, w1, temper, gout, hsc, old, offs, out):
@@ -34,113 +37,114 @@ def tile_attend_blrshared_soft_kernel(tc, query, keys_words, keys_scales, tab_wo
         sb = ctx.enter_context(tc.tile_pool(name="sb", bufs=1))
         ps = ctx.enter_context(tc.psum_pool(name="ps", bufs=1))
 
-        def scale_pool(name, src, tag, clearer, queue):
-            plane = sb.tile([P, T], U8, name=name, tag=tag, align_bytes=64)
+        def load_plane(name, scale_rows, clearer):
+            plane = sb.tile([P, T], U8, name=name, align_bytes=ALIGN)
             clearer.memset(plane[:].bitcast(I32), 0)
-            for quad in range(4):
-                queue.dma_start(out=plane[32 * quad : 32 * quad + 4, :].bitcast(I32), in_=src[0, 4 * quad : 4 * quad + 4, :].bitcast(I32))
+            for quad in range(P // QUADRANT):
+                nc.sync.dma_start(out=plane[QUADRANT * quad : QUADRANT * quad + 4, :].bitcast(I32), in_=scale_rows[0, 4 * quad : 4 * quad + 4, :].bitcast(I32))
             return plane
 
-        def word_pool(name, src, tag):
-            words = sb.tile([P, T], U32, name=name, tag=tag, align_bytes=64)
-            nc.sync.dma_start(out=words[:].bitcast(I32), in_=src[0].rearrange("p n t -> p (n t)").bitcast(I32))
+        def load_words(name, packed, tag):
+            words = sb.tile([P, T], U32, name=name, tag=tag, align_bytes=ALIGN)
+            nc.sync.dma_start(out=words[:].bitcast(I32), in_=packed[0].rearrange("p n t -> p (n t)").bitcast(I32))
             return words
 
+        def load_rows(name, rows, tag):
+            raw = sb.tile([P, PACK, rows.shape[1]], F32, name=name, tag=tag, align_bytes=ALIGN)
+            nc.sync.dma_start(out=raw[:], in_=rows.rearrange("(p t) c -> p t c", t=PACK))
+            return raw
+
+        def interleave(name, raw, copy):
+            grouped = sb.tile([P, Q, PACK], BF16, name=name, align_bytes=ALIGN)
+            copy(out=grouped[:].rearrange("p (c i) t -> p c t i", i=4), in_=raw[:].rearrange("p t (c i) -> p c t i", i=4))
+            return grouped[:].rearrange("p c t -> p (c t)")
+
         def quantise(name, grouped, width):
-            codes = sb.tile([P, width], U32, name=name + "_codes", align_bytes=64)
-            scales = sb.tile([P, width], U8, name=name + "_scales", align_bytes=64)
+            codes = sb.tile([P, width], U32, name=name + "_codes", align_bytes=ALIGN)
+            scales = sb.tile([P, width], U8, name=name + "_scales", align_bytes=ALIGN)
             nc.vector.quantize_mx(out=codes[:].bitcast(FP8X4), scales=scales[:], in_=grouped)
             return codes, scales
 
-        offsets = lists.tile([P, I // 16], U16, name="offsets")
-        tab_plane = scale_pool("tab_plane", tab_scales, "tab_plane", nc.gpsimd, nc.sync)
+        def product(bank, lhs_codes, lhs_scales, rhs_codes, rhs_scales):
+            nc.tensor.matmul_mx(out=bank, lhsT=lhs_codes.bitcast(FP8X4), lhsT_scale=lhs_scales, rhs=rhs_codes.bitcast(FP8X4), rhs_scale=rhs_scales, start=True, stop=True)
+
+        def half(h):
+            return slice(h * HALF_SLOTS, (h + 1) * HALF_SLOTS)
+
+        offsets = lists.tile([P, I // LIST_COLUMN], U16, name="offsets")
+        tab_plane = load_plane("tab_plane", tab_scales, nc.gpsimd)
         nc.sync.dma_start(offsets[:], offs)
-        w1_raw = sb.tile([P, PACK, R], F32, name="w1_raw")
-        nc.sync.dma_start(out=w1_raw[:], in_=w1.rearrange("(p j) r -> p j r", j=PACK))
-        temper_sb = sb.tile([P, PACK], F32, name="temper_sb")
-        nc.sync.dma_start(out=temper_sb[:], in_=temper.rearrange("(p t) o -> p (t o)", t=PACK))
-        hsc_sb = sb.tile([P, PACK], F32, name="hsc_sb", tag="hsc_keys_old", align_bytes=64)
-        nc.sync.dma_start(out=hsc_sb[:], in_=hsc.rearrange("(p t) o -> p (t o)", t=PACK))
-        tab_pool = word_pool("tab_pool", tab_words, "tab_pool")
-        q_raw = sb.tile([P, PACK, Q], F32, name="q_raw")
-        nc.sync.dma_start(out=q_raw[:], in_=query.rearrange("(p j) q -> p j q", j=PACK))
-        keys_plane = scale_pool("keys_plane", keys_scales, "keys_plane", nc.vector, nc.sync)
+        w1_raw = load_rows("w1_raw", w1, "w1_raw")
+        temper_sb = load_rows("temper_sb", temper, "temper_sb")
+        hsc_sb = load_rows("hsc_sb", hsc, "after_hsc")
+        tab_pool = load_words("tab_pool", tab_words, "after_tab")
+        q_raw = load_rows("q_raw", query, "q_raw")
+        keys_plane = load_plane("keys_plane", keys_scales, nc.vector)
         hsc4 = sb.tile([P, PACK], F32, name="hsc4")
-        nc.scalar.activation(out=hsc4[:], in_=hsc_sb[:], func=ACT.Copy, scale=4.0)
-        keys_pool = word_pool("keys_pool", keys_words, "hsc_keys_old")
+        nc.scalar.activation(out=hsc4[:], in_=hsc_sb[:, :, 0], func=ACT.Copy, scale=4.0)
+        keys_pool = load_words("keys_pool", keys_words, "after_hsc")
         ident = sb.tile([P, P], F32, name="ident")
         make_identity(nc, ident[:])
         placed = sb.tile([P, T], F32, name="placed")
         nc.vector.memset(placed[:], 0.0)
 
-        w1_view = w1_raw[:].rearrange("p j (m t) -> p m j t", t=PACK)
-        w1_q = []
-        for pair, eng in enumerate((nc.scalar.copy, nc.vector.tensor_copy)):
-            grouped = sb.tile([P, 2, P, PACK], BF16, name="w1_grouped%d" % pair, tag="w1_grouped%d" % pair, align_bytes=64)
-            eng(out=grouped[:].rearrange("p t m j -> p m j t"), in_=w1_view[:, :, :, 2 * pair : 2 * pair + 2])
-            w1_q.append(quantise("w1_%d" % pair, grouped[:].rearrange("p t m j -> p (t m j)"), 2 * P))
-
-        g_raw = sb.tile([P, PACK, Q], F32, name="g_raw", tag="w1_grouped0", align_bytes=64)
-        nc.sync.dma_start(out=g_raw[:], in_=gout.rearrange("(p j) q -> p j q", j=PACK))
+        w1_dealt = w1_raw[:].rearrange("p s (m t) -> p m s t", t=PACK)
+        w1_mx = []
+        for pair, copy in enumerate((nc.scalar.copy, nc.vector.tensor_copy)):
+            w1_grouped = sb.tile([P, 2, P, PACK], BF16, name="w1_grouped%d" % pair, tag="after_w1_%d" % pair, align_bytes=ALIGN)
+            copy(out=w1_grouped[:].rearrange("p t m s -> p m s t"), in_=w1_dealt[:, :, :, 2 * pair : 2 * pair + 2])
+            w1_mx.append(quantise("w1_%d" % pair, w1_grouped[:].rearrange("p t m s -> p (t m s)"), 2 * P))
+        g_raw = load_rows("g_raw", gout, "after_w1_0")
 
         zh = [ps.tile([P, I], F32, name="zh%d" % t) for t in range(PACK)]
         ht = []
         for h in range(HALVES):
-            picks = offsets[:, h * HS // 16 : (h + 1) * HS // 16]
-            tab_sc = sb.tile([P, HS], U8, name="tab_sc%d" % h, align_bytes=64)
+            picks = offsets[:, h * HALF_SLOTS // LIST_COLUMN : (h + 1) * HALF_SLOTS // LIST_COLUMN]
+            tab_sc = sb.tile([P, HALF_SLOTS], U8, name="tab_sc%d" % h, align_bytes=ALIGN)
             nc.vector.tensor_copy(tab_sc[:], tab_plane[:].indirect(picks))
-            tab_w = sb.tile([P, HS], U32, name="tab_w%d" % h, align_bytes=64)
+            tab_w = sb.tile([P, HALF_SLOTS], U32, name="tab_w%d" % h, align_bytes=ALIGN)
             nc.vector.tensor_copy(tab_w[:], tab_pool[:].indirect(picks))
-            e = sb.tile([P, GROUP, PACK, HG], F32, name="ht%d" % h)
+            ht_half = sb.tile([P, GROUP, PACK, HALF_GROUPS], F32, name="ht%d" % h)
             for t in range(PACK):
-                codes, scales = w1_q[t // 2]
-                cols = slice((t % 2) * P, (t % 2 + 1) * P)
-                nc.tensor.matmul_mx(out=zh[t][:, h * HS : (h + 1) * HS], lhsT=codes[:, cols].bitcast(FP8X4), lhsT_scale=scales[:, cols],
-                                    rhs=tab_w[:].bitcast(FP8X4), rhs_scale=tab_sc[:], start=True, stop=True)
-                nc.scalar.activation(out=e[:, :, t, :], in_=zh[t][:, h * HS : (h + 1) * HS].rearrange("p (g j) -> p j g", j=GROUP),
-                                     func=ACT.Exp, scale=temper_sb[:, t : t + 1])
-            ht.append(e)
-
-        def interleave(name, raw, copy):
-            grouped = sb.tile([P, Q, PACK], BF16, name=name, align_bytes=64)
-            copy(out=grouped[:].rearrange("p (c i) j -> p c j i", i=4), in_=raw[:].rearrange("p j (c i) -> p c j i", i=4))
-            return grouped[:].rearrange("p q j -> p (q j)")
+                w1_codes, w1_scales = w1_mx[t // 2]
+                tile_cols = slice((t % 2) * P, (t % 2 + 1) * P)
+                product(zh[t][:, half(h)], w1_codes[:, tile_cols], w1_scales[:, tile_cols], tab_w[:], tab_sc[:])
+                nc.scalar.activation(out=ht_half[:, :, t, :], in_=zh[t][:, half(h)].rearrange("p (g j) -> p j g", j=GROUP), func=ACT.Exp, scale=temper_sb[:, t, :])
+            ht.append(ht_half)
 
         q_codes, q_scales = quantise("q", interleave("q_grouped", q_raw, nc.vector.tensor_copy), Q)
-
-        keys_sc = sb.tile([P, I], U8, name="keys_sc", tag="tab_pool", align_bytes=64)
+        keys_sc = sb.tile([P, I], U8, name="keys_sc", tag="after_tab", align_bytes=ALIGN)
         nc.vector.tensor_copy(keys_sc[:], keys_plane[:].indirect(offsets[:]))
-        keys_w = sb.tile([P, I], U32, name="keys_w", align_bytes=64)
+        keys_w = sb.tile([P, I], U32, name="keys_w", align_bytes=ALIGN)
         nc.vector.tensor_copy(keys_w[:], keys_pool[:].indirect(offsets[:]))
 
-        sums = []
+        group_bank = []
         for h in range(HALVES):
-            bank = ps.tile([P, 2, P], F32, name="sums%d" % h)
+            bank = ps.tile([P, 2, P], F32, name="group_bank%d" % h)
             for j in range(GROUP):
-                nc.tensor.matmul(out=bank[:, 0, :], lhsT=ht[h][:, j, :, :].rearrange("p t g -> p (t g)"), rhs=ident[:],
-                                 is_transpose=True, start=(j == 0), stop=(j == GROUP - 1))
-            sums.append(bank)
+                nc.tensor.matmul(out=bank[:, 0, :], lhsT=ht[h][:, j, :, :].rearrange("p t g -> p (t g)"), rhs=ident[:], is_transpose=True, start=(j == 0), stop=(j == GROUP - 1))
+            group_bank.append(bank)
 
         a = ps.tile([P, I], F32, name="a")
-        nc.tensor.matmul_mx(out=a[:], lhsT=q_codes[:].bitcast(FP8X4), lhsT_scale=q_scales[:], rhs=keys_w[:].bitcast(FP8X4), rhs_scale=keys_sc[:], start=True, stop=True)
+        product(a[:], q_codes[:], q_scales[:], keys_w[:], keys_sc[:])
 
-        hts = []
+        ht_scaled = []
+        rec_turned = sb.tile([P, HALVES, P], F32, name="rec_turned", tag="after_hsc", align_bytes=ALIGN)
         for h in range(HALVES):
-            rec_t = sb.tile([P, P], F32, name="rec_t%d" % h, tag="hsc_keys_old", align_bytes=64)
-            nc.vector.reciprocal(out=rec_t[:], in_=sums[h][:, 0, :])
-            nc.tensor.transpose(sums[h][:, 1, :], rec_t[:], ident[:])
-            s = sb.tile([P, PAIRS, PACK, HG, 2], F32, name="hts%d" % h)
+            nc.vector.reciprocal(out=rec_turned[:, h, :], in_=group_bank[h][:, 0, :])
+            nc.tensor.transpose(group_bank[h][:, 1, :], rec_turned[:, h, :], ident[:])
+            scaled = sb.tile([P, PAIRS, PACK, HALF_GROUPS, 2], F32, name="ht_scaled%d" % h)
             for t in range(PACK):
-                nc.scalar.activation(out=s[:, :, t, :, :], in_=ht[h][:, :, t, :].rearrange("p (u e) g -> p u g e", e=2), func=ACT.Copy, scale=hsc4[:, t : t + 1])
-            hts.append(s)
-            if h == 0:
-                nmax = sb.tile([P, 1], F32, name="nmax")
-                nc.vector.tensor_reduce(out=nmax[:], in_=a[:], axis=AX.X, op=ALU.max, negate=True)
-                p = sb.tile([P, I], F32, name="p")
-                z = sb.tile([P, 1], F32, name="z")
-                nc.scalar.activation(out=p[:], in_=a[:], func=ACT.Exp, bias=nmax[:], scale=1.0, accum_out=z[:])
+                nc.scalar.activation(out=scaled[:, :, t, :, :], in_=ht[h][:, :, t, :].rearrange("p (u e) g -> p u g e", e=2), func=ACT.Copy, scale=hsc4[:, t : t + 1])
+            ht_scaled.append(scaled)
 
-        old_sb = sb.tile([P, T], F32, name="old_sb", tag="hsc_keys_old", align_bytes=64)
+        neg_max = sb.tile([P, 1], F32, name="neg_max")
+        nc.vector.tensor_reduce(out=neg_max[:], in_=a[:], axis=AX.X, op=ALU.max, negate=True)
+        p = sb.tile([P, I], F32, name="p")
+        z = sb.tile([P, 1], F32, name="z")
+        nc.scalar.activation(out=p[:], in_=a[:], func=ACT.Exp, bias=neg_max[:], scale=1.0, accum_out=z[:])
+
+        old_sb = sb.tile([P, T], F32, name="old_sb", tag="after_hsc", align_bytes=ALIGN)
         nc.sync.dma_start(out=old_sb[:], in_=old)
 
         g_codes, g_scales = quantise("g", interleave("g_grouped", g_raw, nc.scalar.copy), Q)
@@ -149,39 +153,39 @@ def tile_attend_blrshared_soft_kernel(tc, query, keys_words, keys_scales, tab_wo
         nc.vector.reciprocal(out=rz[:], in_=z[:])
         rz512 = sb.tile([P, 1], F32, name="rz512")
         nc.scalar.activation(out=rz512[:], in_=rz[:], func=ACT.Copy, scale=512.0)
-
-        p_dealt = sb.tile([P, PAIRS, HG, 2], F32, name="p_dealt")
-        nc.scalar.copy(out=p_dealt[:], in_=p[:, HS:].rearrange("p (g u e) -> p u g e", u=PAIRS, e=2))
-        pa = sb.tile([P, I], F32, name="pa")
-        nc.scalar.activation(out=pa[:], in_=p[:], func=ACT.Copy, scale=rz512[:])
+        p_dealt = sb.tile([P, PAIRS, HALF_GROUPS, 2], F32, name="p_dealt")
+        nc.scalar.copy(out=p_dealt[:], in_=p[:, half(1)].rearrange("p (g u e) -> p u g e", u=PAIRS, e=2))
+        weight = sb.tile([P, I], F32, name="weight")
+        nc.scalar.activation(out=weight[:], in_=p[:], func=ACT.Copy, scale=rz512[:])
 
         c0 = []
         for h in range(HALVES):
-            grouped = sb.tile([P, PAIRS, HG, 2, PACK], BF16, name="hs%d" % h, tag="hs%d" % h, align_bytes=64)
-            rec = sums[h][:, 1, :].rearrange("p (t g) -> p g t", t=PACK).unsqueeze(3).to_broadcast([P, HG, PACK, 2])
+            hs1 = sb.tile([P, PAIRS, HALF_GROUPS, 2, PACK], BF16, name="hs1_%d" % h, tag="after_hs1_%d" % h, align_bytes=ALIGN)
+            rec = group_bank[h][:, 1, :].rearrange("p (t g) -> p g t", t=PACK).unsqueeze(3).to_broadcast([P, HALF_GROUPS, PACK, 2])
             for u in range(PAIRS):
-                nc.vector.tensor_tensor(out=grouped[:, u].rearrange("p g e t -> p g t e"), in0=hts[h][:, u].rearrange("p t g e -> p g t e"), in1=rec, op=ALU.mult)
-            codes, scales = quantise("hs%d" % h, grouped[:].rearrange("p u g e t -> p (u g e t)"), HS)
-            bank = ps.tile([P, HS], F32, name="c0_%d" % h, tag=("c0", "zh0")[h])
-            nc.tensor.matmul_mx(out=bank[:], lhsT=g_codes[:].bitcast(FP8X4), lhsT_scale=g_scales[:], rhs=codes[:].bitcast(FP8X4), rhs_scale=scales[:], start=True, stop=True)
-            c0.append(bank)
+                nc.vector.tensor_tensor(out=hs1[:, u].rearrange("p g e t -> p g t e"), in0=ht_scaled[h][:, u].rearrange("p t g e -> p g t e"), in1=rec, op=ALU.mult)
+            hs1_codes, hs1_scales = quantise("hs1_%d" % h, hs1[:].rearrange("p u g e t -> p (u g e t)"), HALF_SLOTS)
+            c0_half = ps.tile([P, HALF_SLOTS], F32, name="c0_%d" % h, tag=("c0", "zh0")[h])
+            product(c0_half[:], g_codes[:], g_scales[:], hs1_codes[:], hs1_scales[:])
+            c0.append(c0_half)
 
-        by_slot = [bank[:].rearrange("p (u g e) -> p g u e", u=PAIRS, e=2) for bank in c0]
-        c0_first = sb.tile([P, HS], F32, name="c0_first")
-        nc.scalar.copy(out=c0_first[:].rearrange("p (g u e) -> p g u e", u=PAIRS, e=2), in_=by_slot[0])
-        prod = sb.tile([P, HALVES, HS], F32, name="prod", tag="hs1", align_bytes=64)
-        shift = []
-        for h, (values, weights) in enumerate(((c0_first[:], p[:, :HS]), (c0[1][:], p_dealt[:].rearrange("p u g e -> p (u g e)")))):
-            part = sb.tile([P, 1], F32, name="part%d" % h)
-            nc.vector.scalar_tensor_tensor(out=prod[:, h, :], in0=values, scalar=rz[:], in1=weights, op0=ALU.mult, op1=ALU.mult, accum_out=part[:])
-            shift.append(part)
-        d = sb.tile([P, I], F32, name="d")
-        nc.vector.tensor_scalar(out=d[:, :HS], in0=c0_first[:], scalar1=shift[0][:], scalar2=shift[1][:], op0=ALU.subtract, op1=ALU.subtract)
-        nc.vector.tensor_scalar(out=d[:, HS:].rearrange("p (g u e) -> p g u e", u=PAIRS, e=2), in0=by_slot[1], scalar1=shift[0][:], scalar2=shift[1][:], op0=ALU.subtract, op1=ALU.subtract)
-        nc.vector.tensor_tensor(placed[:].indirect(offsets[:]), d[:], pa[:], ALU.mult)
+        c0_by_slot = [c0_half[:].rearrange("p (u g e) -> p g u e", u=PAIRS, e=2) for c0_half in c0]
+        c0_first = sb.tile([P, HALF_SLOTS], F32, name="c0_first")
+        nc.scalar.copy(out=c0_first[:].rearrange("p (g u e) -> p g u e", u=PAIRS, e=2), in_=c0_by_slot[0])
+        terms = sb.tile([P, HALVES, HALF_SLOTS], F32, name="terms", tag="after_hs1_1", align_bytes=ALIGN)
+        row_sums = []
+        for h, (values, probs) in enumerate(((c0_first[:], p[:, half(0)]), (c0[1][:], p_dealt[:].rearrange("p u g e -> p (u g e)")))):
+            row_sum = sb.tile([P, 1], F32, name="row_sum%d" % h)
+            nc.vector.scalar_tensor_tensor(out=terms[:, h, :], in0=values, scalar=rz[:], in1=probs, op0=ALU.mult, op1=ALU.mult, accum_out=row_sum[:])
+            row_sums.append(row_sum)
+        centred = sb.tile([P, I], F32, name="centred")
+        nc.vector.tensor_scalar(out=centred[:, half(0)], in0=c0_first[:], scalar1=row_sums[0][:], scalar2=row_sums[1][:], op0=ALU.subtract, op1=ALU.subtract)
+        nc.vector.tensor_scalar(out=centred[:, half(1)].rearrange("p (g u e) -> p g u e", u=PAIRS, e=2), in0=c0_by_slot[1],
+                                scalar1=row_sums[0][:], scalar2=row_sums[1][:], op0=ALU.subtract, op1=ALU.subtract)
+        nc.vector.tensor_tensor(placed[:].indirect(offsets[:]), centred[:], weight[:], ALU.mult)
 
         for c in range(len(STORE_EDGES) - 1):
             cols = slice(STORE_EDGES[c], STORE_EDGES[c + 1])
-            res = sb.tile([P, STORE_EDGES[c + 1] - STORE_EDGES[c]], F32, name="res%d" % c)
-            nc.vector.tensor_tensor(out=res[:], in0=placed[:, cols], in1=old_sb[:, cols], op=ALU.add)
-            nc.sync.dma_start(out=out[:, cols], in_=res[:])
+            result = sb.tile([P, cols.stop - cols.start], F32, name="result%d" % c)
+            nc.vector.tensor_tensor(out=result[:], in0=placed[:, cols], in1=old_sb[:, cols], op=ALU.add)
+            nc.sync.dma_start(out=out[:, cols], in_=result[:])

from contextlib import ExitStack

import concourse.mybir as mybir
from concourse.masks import make_identity

D, K, R, T, I, Q, G = 512, 512, 512, 2048, 512, 128, 64
FLOPS = 2 * (D * Q * I + K * R * I + R * Q * I)

F32 = mybir.dt.float32
BF16 = mybir.dt.bfloat16
I32 = mybir.dt.int32
U32 = mybir.dt.uint32
U16 = mybir.dt.uint16
U8 = mybir.dt.uint8
FP8X4 = mybir.dt.float8_e4m3fn_x4
ALU = mybir.AluOpType
ACT = mybir.ActivationFunctionType
AX = mybir.AxisListType

P = 128
PACK = 4
QUADRANT = 32
LIST_COLUMN = 16
ALIGN = 64
GROUP = I // G
PAIRS = GROUP // 2
HALVES = 2
HALF_SLOTS = I // HALVES
HALF_GROUPS = G // HALVES
STORE_EDGES = [0, 256, 704, 1152, 1600, 2048]


def tile_attend_blrshared_soft_kernel(tc, query, keys_words, keys_scales, tab_words, tab_scales, w1, temper, gout, hsc, old, offs, out):
    nc = tc.nc
    with ExitStack() as ctx:
        lists = ctx.enter_context(tc.tile_pool(name="lists", bufs=1))
        sb = ctx.enter_context(tc.tile_pool(name="sb", bufs=1))
        ps = ctx.enter_context(tc.psum_pool(name="ps", bufs=1))

        def load_plane(name, scale_rows, clearer):
            plane = sb.tile([P, T], U8, name=name, align_bytes=ALIGN)
            clearer.memset(plane[:].bitcast(I32), 0)
            for quad in range(P // QUADRANT):
                nc.sync.dma_start(out=plane[QUADRANT * quad : QUADRANT * quad + 4, :].bitcast(I32), in_=scale_rows[0, 4 * quad : 4 * quad + 4, :].bitcast(I32))
            return plane

        def load_words(name, packed, tag):
            words = sb.tile([P, T], U32, name=name, tag=tag, align_bytes=ALIGN)
            nc.sync.dma_start(out=words[:].bitcast(I32), in_=packed[0].rearrange("p n t -> p (n t)").bitcast(I32))
            return words

        def load_rows(name, rows, tag):
            raw = sb.tile([P, PACK, rows.shape[1]], F32, name=name, tag=tag, align_bytes=ALIGN)
            nc.sync.dma_start(out=raw[:], in_=rows.rearrange("(p t) c -> p t c", t=PACK))
            return raw

        def interleave(name, raw, copy):
            grouped = sb.tile([P, Q, PACK], BF16, name=name, align_bytes=ALIGN)
            copy(out=grouped[:].rearrange("p (c i) t -> p c t i", i=4), in_=raw[:].rearrange("p t (c i) -> p c t i", i=4))
            return grouped[:].rearrange("p c t -> p (c t)")

        def quantise(name, grouped, width):
            codes = sb.tile([P, width], U32, name=name + "_codes", align_bytes=ALIGN)
            scales = sb.tile([P, width], U8, name=name + "_scales", align_bytes=ALIGN)
            nc.vector.quantize_mx(out=codes[:].bitcast(FP8X4), scales=scales[:], in_=grouped)
            return codes, scales

        def product(bank, lhs_codes, lhs_scales, rhs_codes, rhs_scales):
            nc.tensor.matmul_mx(out=bank, lhsT=lhs_codes.bitcast(FP8X4), lhsT_scale=lhs_scales, rhs=rhs_codes.bitcast(FP8X4), rhs_scale=rhs_scales, start=True, stop=True)

        def half(h):
            return slice(h * HALF_SLOTS, (h + 1) * HALF_SLOTS)

        offsets = lists.tile([P, I // LIST_COLUMN], U16, name="offsets")
        tab_plane = load_plane("tab_plane", tab_scales, nc.gpsimd)
        nc.sync.dma_start(offsets[:], offs)
        w1_raw = load_rows("w1_raw", w1, "w1_raw")
        temper_sb = load_rows("temper_sb", temper, "temper_sb")
        hsc_sb = load_rows("hsc_sb", hsc, "after_hsc")
        tab_pool = load_words("tab_pool", tab_words, "after_tab")
        q_raw = load_rows("q_raw", query, "q_raw")
        keys_plane = load_plane("keys_plane", keys_scales, nc.vector)
        hsc4 = sb.tile([P, PACK], F32, name="hsc4")
        nc.scalar.activation(out=hsc4[:], in_=hsc_sb[:, :, 0], func=ACT.Copy, scale=4.0)
        keys_pool = load_words("keys_pool", keys_words, "after_hsc")
        ident = sb.tile([P, P], F32, name="ident")
        make_identity(nc, ident[:])
        placed = sb.tile([P, T], F32, name="placed")
        nc.vector.memset(placed[:], 0.0)

        w1_dealt = w1_raw[:].rearrange("p s (m t) -> p m s t", t=PACK)
        w1_mx = []
        for pair, copy in enumerate((nc.scalar.copy, nc.vector.tensor_copy)):
            w1_grouped = sb.tile([P, 2, P, PACK], BF16, name="w1_grouped%d" % pair, tag="after_w1_%d" % pair, align_bytes=ALIGN)
            copy(out=w1_grouped[:].rearrange("p t m s -> p m s t"), in_=w1_dealt[:, :, :, 2 * pair : 2 * pair + 2])
            w1_mx.append(quantise("w1_%d" % pair, w1_grouped[:].rearrange("p t m s -> p (t m s)"), 2 * P))
        g_raw = load_rows("g_raw", gout, "after_w1_0")

        zh = [ps.tile([P, I], F32, name="zh%d" % t) for t in range(PACK)]
        ht = []
        for h in range(HALVES):
            picks = offsets[:, h * HALF_SLOTS // LIST_COLUMN : (h + 1) * HALF_SLOTS // LIST_COLUMN]
            tab_sc = sb.tile([P, HALF_SLOTS], U8, name="tab_sc%d" % h, align_bytes=ALIGN)
            nc.vector.tensor_copy(tab_sc[:], tab_plane[:].indirect(picks))
            tab_w = sb.tile([P, HALF_SLOTS], U32, name="tab_w%d" % h, align_bytes=ALIGN)
            nc.vector.tensor_copy(tab_w[:], tab_pool[:].indirect(picks))
            ht_half = sb.tile([P, GROUP, PACK, HALF_GROUPS], F32, name="ht%d" % h)
            for t in range(PACK):
                w1_codes, w1_scales = w1_mx[t // 2]
                tile_cols = slice((t % 2) * P, (t % 2 + 1) * P)
                product(zh[t][:, half(h)], w1_codes[:, tile_cols], w1_scales[:, tile_cols], tab_w[:], tab_sc[:])
                nc.scalar.activation(out=ht_half[:, :, t, :], in_=zh[t][:, half(h)].rearrange("p (g j) -> p j g", j=GROUP), func=ACT.Exp, scale=temper_sb[:, t, :])
            ht.append(ht_half)

        q_codes, q_scales = quantise("q", interleave("q_grouped", q_raw, nc.vector.tensor_copy), Q)
        keys_sc = sb.tile([P, I], U8, name="keys_sc", tag="after_tab", align_bytes=ALIGN)
        nc.vector.tensor_copy(keys_sc[:], keys_plane[:].indirect(offsets[:]))
        keys_w = sb.tile([P, I], U32, name="keys_w", align_bytes=ALIGN)
        nc.vector.tensor_copy(keys_w[:], keys_pool[:].indirect(offsets[:]))

        group_bank = []
        for h in range(HALVES):
            bank = ps.tile([P, 2, P], F32, name="group_bank%d" % h)
            for j in range(GROUP):
                nc.tensor.matmul(out=bank[:, 0, :], lhsT=ht[h][:, j, :, :].rearrange("p t g -> p (t g)"), rhs=ident[:], is_transpose=True, start=(j == 0), stop=(j == GROUP - 1))
            group_bank.append(bank)

        a = ps.tile([P, I], F32, name="a")
        product(a[:], q_codes[:], q_scales[:], keys_w[:], keys_sc[:])

        ht_scaled = []
        rec_turned = sb.tile([P, HALVES, P], F32, name="rec_turned", tag="after_hsc", align_bytes=ALIGN)
        for h in range(HALVES):
            nc.vector.reciprocal(out=rec_turned[:, h, :], in_=group_bank[h][:, 0, :])
            nc.tensor.transpose(group_bank[h][:, 1, :], rec_turned[:, h, :], ident[:])
            scaled = sb.tile([P, PAIRS, PACK, HALF_GROUPS, 2], F32, name="ht_scaled%d" % h)
            for t in range(PACK):
                nc.scalar.activation(out=scaled[:, :, t, :, :], in_=ht[h][:, :, t, :].rearrange("p (u e) g -> p u g e", e=2), func=ACT.Copy, scale=hsc4[:, t : t + 1])
            ht_scaled.append(scaled)

        neg_max = sb.tile([P, 1], F32, name="neg_max")
        nc.vector.tensor_reduce(out=neg_max[:], in_=a[:], axis=AX.X, op=ALU.max, negate=True)
        p = sb.tile([P, I], F32, name="p")
        z = sb.tile([P, 1], F32, name="z")
        nc.scalar.activation(out=p[:], in_=a[:], func=ACT.Exp, bias=neg_max[:], scale=1.0, accum_out=z[:])

        old_sb = sb.tile([P, T], F32, name="old_sb", tag="after_hsc", align_bytes=ALIGN)
        nc.sync.dma_start(out=old_sb[:], in_=old)

        g_codes, g_scales = quantise("g", interleave("g_grouped", g_raw, nc.scalar.copy), Q)

        rz = sb.tile([P, 1], F32, name="rz")
        nc.vector.reciprocal(out=rz[:], in_=z[:])
        rz512 = sb.tile([P, 1], F32, name="rz512")
        nc.scalar.activation(out=rz512[:], in_=rz[:], func=ACT.Copy, scale=512.0)
        p_dealt = sb.tile([P, PAIRS, HALF_GROUPS, 2], F32, name="p_dealt")
        nc.scalar.copy(out=p_dealt[:], in_=p[:, half(1)].rearrange("p (g u e) -> p u g e", u=PAIRS, e=2))
        weight = sb.tile([P, I], F32, name="weight")
        nc.scalar.activation(out=weight[:], in_=p[:], func=ACT.Copy, scale=rz512[:])

        c0 = []
        for h in range(HALVES):
            hs1 = sb.tile([P, PAIRS, HALF_GROUPS, 2, PACK], BF16, name="hs1_%d" % h, tag="after_hs1_%d" % h, align_bytes=ALIGN)
            rec = group_bank[h][:, 1, :].rearrange("p (t g) -> p g t", t=PACK).unsqueeze(3).to_broadcast([P, HALF_GROUPS, PACK, 2])
            for u in range(PAIRS):
                nc.vector.tensor_tensor(out=hs1[:, u].rearrange("p g e t -> p g t e"), in0=ht_scaled[h][:, u].rearrange("p t g e -> p g t e"), in1=rec, op=ALU.mult)
            hs1_codes, hs1_scales = quantise("hs1_%d" % h, hs1[:].rearrange("p u g e t -> p (u g e t)"), HALF_SLOTS)
            c0_half = ps.tile([P, HALF_SLOTS], F32, name="c0_%d" % h, tag=("c0", "zh0")[h])
            product(c0_half[:], g_codes[:], g_scales[:], hs1_codes[:], hs1_scales[:])
            c0.append(c0_half)

        c0_by_slot = [c0_half[:].rearrange("p (u g e) -> p g u e", u=PAIRS, e=2) for c0_half in c0]
        c0_first = sb.tile([P, HALF_SLOTS], F32, name="c0_first")
        nc.scalar.copy(out=c0_first[:].rearrange("p (g u e) -> p g u e", u=PAIRS, e=2), in_=c0_by_slot[0])
        terms = sb.tile([P, HALVES, HALF_SLOTS], F32, name="terms", tag="after_hs1_1", align_bytes=ALIGN)
        row_sums = []
        for h, (values, probs) in enumerate(((c0_first[:], p[:, half(0)]), (c0[1][:], p_dealt[:].rearrange("p u g e -> p (u g e)")))):
            row_sum = sb.tile([P, 1], F32, name="row_sum%d" % h)
            nc.vector.scalar_tensor_tensor(out=terms[:, h, :], in0=values, scalar=rz[:], in1=probs, op0=ALU.mult, op1=ALU.mult, accum_out=row_sum[:])
            row_sums.append(row_sum)
        centred = sb.tile([P, I], F32, name="centred")
        nc.vector.tensor_scalar(out=centred[:, half(0)], in0=c0_first[:], scalar1=row_sums[0][:], scalar2=row_sums[1][:], op0=ALU.subtract, op1=ALU.subtract)
        nc.vector.tensor_scalar(out=centred[:, half(1)].rearrange("p (g u e) -> p g u e", u=PAIRS, e=2), in0=c0_by_slot[1],
                                scalar1=row_sums[0][:], scalar2=row_sums[1][:], op0=ALU.subtract, op1=ALU.subtract)
        nc.vector.tensor_tensor(placed[:].indirect(offsets[:]), centred[:], weight[:], ALU.mult)

        for c in range(len(STORE_EDGES) - 1):
            cols = slice(STORE_EDGES[c], STORE_EDGES[c + 1])
            result = sb.tile([P, cols.stop - cols.start], F32, name="result%d" % c)
            nc.vector.tensor_tensor(out=result[:], in0=placed[:, cols], in1=old_sb[:, cols], op=ALU.add)
            nc.sync.dma_start(out=out[:, cols], in_=result[:])
